import numpy as np, ml_dtypes
CORES = [23,119,17,113]
N = 4
BF = ml_dtypes.bfloat16
def gentries(a):
    return np.ascontiguousarray(a.reshape(8, 16, -1).transpose(0, 2, 1)).reshape(8, -1)
def gtable(e):
    e = np.asarray(e); return np.ascontiguousarray(e.reshape(8, -1, 16).transpose(0, 2, 1)).reshape(128, -1).astype(np.int32)
V, R, M, RO, P, H, CAP, NEED = 4096, 2048, 3, 3, 6, 2, 256, 9
S, TOP = V // N, 2 ** 20 - 1
def parts(rng):
    base = rng.integers(0, 2 ** 20, (1, 8, 16, 1)); amp = np.exp2(10 + 7 * rng.random((N, 8, 1, R)))
    x = np.clip(base + amp * rng.standard_normal((N, 8, 16, R)), 0, TOP).astype(np.int64)
    t = (np.exp2(14 + 3.5 * rng.random((N, 8, 1, 1))) * (0.5 + rng.random((N, 8, 16, 1)))).astype(np.int64)
    lv = rng.integers(0, V, (N, 8, P, R)); lv = np.where(rng.random((N, 8, 1, R)) < 0.5, np.sort(lv, axis=2), lv)
    cd = rng.integers(0, R, (N, 8, RO, M, V))
    return x, t, lv, cd
def pack(x, t, lv, cd):
    return {"px": np.ascontiguousarray(x.reshape(N, 128, R)).astype(np.int32), "th": np.ascontiguousarray(t.reshape(N, 128, 1)).astype(np.int32),
            "ray": np.stack([gtable(a.reshape(8, -1)) for a in lv]), "cand": np.stack([gtable(a.reshape(8, -1)) for a in cd])}
def setup_inputs(rng):
    return pack(*parts(rng))
def setup_inputs_room(rng):
    x, t, lv, cd = parts(rng); h = R // 8
    t = rng.integers(2 ** 14, 2 ** 15, (N, 8, 16, 1)); x = rng.integers(2 ** 18, 2 ** 19, (1, 8, 16, 1)) + rng.integers(0, 2 ** 13, (N, 8, 16, R))
    inc = np.zeros((8, V), bool); own = np.arange(V) // S
    for o in range(N):
        for g in range(8):
            n = int(rng.choice(np.array([0, 1, CAP - 1, CAP, CAP + 1, S]))); last = o == N - 1 and g < 4
            if o == 0: n = (CAP, CAP + 1, S, CAP - 1, 1, 0, CAP, CAP + 1)[g]
            if last: n = (CAP, 1, CAP - 1, CAP)[g]
            s = rng.permutation(S)[:n]
            if last and not np.any(s == S - 1): s[0] = S - 1
            inc[g, o * S + s] = True
    for a in range(N):
        for g in range(8):
            o = rng.permutation(R); hot, watch, calm = o[:h], o[h:2 * h], o[h:]
            m = np.argsort(rng.random((16, h)), axis=0) < rng.integers(NEED, 17, h)
            x[a, g][:, hot] += m * (rng.choice(np.array([-1, 1]), h) * rng.integers(2 ** 16, 2 ** 17, h))
            lv[a, g, 0, o[:2 * h]] = V - 1; cd[a, g, 0] = rng.choice(calm, (M, V))
            for who, back in ((hot, 1), (watch, 2)):
                v = np.flatnonzero(inc[g] & ((own + back) % N == a))
                cd[a, g, 0, rng.integers(0, M, len(v)), v] = rng.choice(who, len(v))
    return pack(x, t, lv, cd)
def setup_inputs_ties(rng):
    x, t, lv, cd = parts(rng); n = min(R // 8, S)
    base = rng.choice(np.array([0, 2 ** 19, TOP]), 8); base[0] = 0; base[1] = TOP; base[2] = 2 ** 19; sg = np.where(base > 2 ** 19, -1, 1)
    t = rng.choice(np.array([0, 1, 1000, 2 ** 18, 2 ** 19 - 8]), (N, 8, 1, 1)) + rng.integers(0, 3, (N, 8, 16, 1))
    x = np.tile(base.reshape(1, 8, 1, 1), (N, 1, 16, R))
    for a in range(N):
        for g in range(8):
            o = rng.permutation(R); hot, watch, calm = o[:n], o[n:2 * n], o[n:]; b, e = (a - 1) % N, (a - 2) % N
            m = (np.argsort(rng.random((16, n)), axis=0) < rng.choice(np.array([NEED - 1, NEED, 16]), n)).astype(np.int64)
            x[a, g][:, hot] = base[g] + sg[g] * (t[b, g] + m)
            v = b * S + rng.permutation(S)[:n]
            lv[a, g, 0, hot] = np.where(rng.random(n) < 0.4, v, np.where(rng.random(n) < 0.5, V - 1, np.maximum(v - 1, 0)))
            lv[a, g, 0, watch] = V - 1
            cd[a, g, 0] = rng.choice(calm, (M, V)); cd[a, g, 0, 0, v] = hot
            cd[a, g, 0, M - 1, e * S:(e + 1) * S] = rng.choice(watch, S)
    return pack(x, t, lv, cd)
def setup_inputs_alike(rng):
    x, t, lv, cd = parts(rng)
    cd[:, ::4] = rng.choice(np.array([0, R - 1, R // 2, 5]), (N, 2, RO, M, V)); cd[:, 3] = cd[:, 3][:, :, :1]
    lv[:, 1::2] = lv[:, 1::2, :1]
    lv[:, 2] = rng.choice(np.array([0, V - 1]), (N, P, R)); lv[:, 6] = rng.integers(0, 16, (N, P, R))
    return pack(x, t, lv, cd)
def setup_inputs_dim(rng):
    x, t, lv, cd = parts(rng); q = rng.permutation(N); k = int(rng.integers(0, 7)); o = int(q[1])
    lv[:, k] = lv[:, k] // 2; lv[q[0], :7] = rng.integers(0, 4, (7, P, R)); t[o] = TOP; t[q[2]] = 0
    for a, pixel in ((int(q[0]), 0), (int(q[3]), TOP)):
        s = rng.permutation(R)[:R // 16]; x[a, 7][:, s] = pixel; lv[a, 7, 0, s] = V - 1
        cd[a, 7, 0, 0, o * S:(o + 1) * S] = rng.choice(s, S)
    return pack(x, t, lv, cd)
def setup_inputs_spread(rng):
    x, t, lv, cd = parts(rng)
    t = np.minimum(np.exp2(10 + 10 * rng.random((N, 8, 16, 1))).astype(np.int64), TOP)
    x = np.minimum((np.exp2(20 * rng.random((N, 8, 1, R))) * rng.random((N, 8, 16, R))).astype(np.int64), TOP)
    return pack(x, t, lv, cd)
def check_inputs(d):
    bad = []
    for k, lo, hi in (("px", 0, TOP), ("th", 0, TOP), ("ray", 0, V - 1), ("cand", 0, R - 1)):
        if np.min(d[k]) < lo or np.max(d[k]) > hi: bad.append("range of " + k)
    return bad
def reference(px, th, ray, cand):
    x = px.astype(np.int64).reshape(N, 8, 16, R); t = th.astype(np.int64).reshape(N, 8, 16, 1)
    lv = np.stack([gentries(a) for a in ray]).astype(np.int64).reshape(N, 8, P, R)
    cd = np.stack([gentries(a) for a in cand]).astype(np.int64).reshape(N, 8, RO, M, V)
    c = np.zeros((N, 8, R), np.int64); number = np.arange(V)
    for rnd in range(RO):
        w = np.take_along_axis(lv, c[:, :, None, :], 2)[:, :, 0]
        lo = np.full((8, 16, V), TOP + 1, np.int64); hi = np.full((8, 16, V), -1, np.int64)
        for a in range(N):
            for m in range(M):
                ix = cd[a, :, rnd, m]
                sees = (number <= np.take_along_axis(w[a], ix, 1))[:, None, :]
                v = np.take_along_axis(x[a], ix[:, None, :], 2)
                lo = np.minimum(lo, np.where(sees, v, TOP + 1)); hi = np.maximum(hi, np.where(sees, v, -1))
        carved = np.zeros((8, V), bool)
        for o in range(N):
            far = (hi[:, :, o * S:(o + 1) * S] - lo[:, :, o * S:(o + 1) * S] > t[o]).astype(np.int64)
            odd = np.add.reduce(far, axis=1) >= NEED
            carved[:, o * S:(o + 1) * S] = odd & (np.add.accumulate(odd.astype(np.int64), axis=1) <= CAP)
        for step in range(H):
            w = np.take_along_axis(lv, c[:, :, None, :], 2)[:, :, 0]
            nx, nc = [], []
            for a in range(N):
                gone = np.take_along_axis(carved, w[a], 1); e = np.take_along_axis(lo, w[a][:, None, :], 2)
                nx.append(np.where(gone[:, None, :], np.clip(x[a] + ((x[a] - e) >> 2), 0, TOP), x[a]))
                nc.append(np.minimum(c[a] + gone.astype(np.int64), P - 1))
            x = np.stack(nx); c = np.stack(nc)
    yc = np.stack([gtable(c[a]) for a in range(N)])
    return {"yx": x.reshape(N, 128, R).astype(np.float32), "yc": yc.astype(np.float32)}

@@ -1,0 +1,456 @@
+from concourse.bass import DstId, RemoteDMATransfer
+from concourse.mybir import AluOpType as A, ActivationFunctionType as F
+
+TOP = 2 ** 20 - 1
+SCRATCH = {}
+
+
+def _buf(where, dtype, **shapes):
+    for n, s in shapes.items():
+        SCRATCH[n] = (where, s if isinstance(s, list) else [128, s], dtype)
+
+
+_buf("dram", "int32", sp=[4, 128, 512], lp=[4, 128, 512], sr=[4, 128, 192], lr=[4, 128, 192], cr=[4, 32, 3, 4, 3, 64], sc=[12, 128, 192])
+_buf("dram", "float32", so=[16, 128, 128], lo=[16, 128, 128], sy=[4, 128, 32], ly=[4, 128, 32])
+_buf("sbuf", "int32", cg0=768, cg1=768, cg2=768, ca=768, xi=2048, rayi=768, tho=1, thl=4, thi=1,
+     zi=256, it0=144, it1=144, vci=384, pc=1, lane=1, grp=1, oi=1, xi4=4, xj4=4, ish=128, im16=128)
+_buf("sbuf", "uint16", lw0=768, lw1=768, lw2=768, lx=768, ln=256, oe=256)
+_buf("sbuf", "bfloat16", wr=12288, fl=1024, m2=128, mcb=144, mid=128, mb2=144, mbc=128, mex=2048, vct=384)
+_buf("sbuf", "float32", xb0=768, xb1=768, xb2=768, thf=1, xw=8192, wt=8192, mt=4096, et=4104, xg=4096, le=384, l1=192, l2=96,
+     l3=32, lm=384, le2=384, lt=1024, odd=64, zz=64, cu=80, cs=80, cv=64, eg=4096, la=768, lb=768, dd=640, zf=256, f1=128, ft=256, fu=128,
+     cc=128, cf=128, lanef=1, grpf=1, of=1, k0=1, nk0=1, g16=1, nb=2, pb=2, colx=4, cole=1, lmk=16, mbo=128, mgt=128, mtri=128)
+_buf("psum", "float32", pA=2048, pB=1024, pC=512, pD=512)
+PSUM = ("pA", "pB", "pC", "pD")
+ENG = {"v": "q_v", "s": "q_s", "t": "q_t", "g": "q_g"}
+DSEM = ["d%d" % j for j in range(64)]
+SEMAPHORES = list(ENG.values()) + DSEM + ["r_ray", "r_c0", "r_px", "r_th", "r_c1", "r_c2", "r_yc", "r_x0", "r_x1", "r_x2", "r_x3", "r_loc"]
+VSHARE = (0, 1)
+CHUNKS = ((0, 1024), (1024, 1536), (1536, 2048))
+CHUNKS_END = ((0, 512), (512, 1024), (1024, 1536), (1536, 2048))
+
+
+def rank_program(g, core, T, topo):
+    me = T.rank_of(core)
+    if me is None:
+        return
+    Q = {"v": g.vector, "s": g.scalar, "t": g.tensor, "y": g.sync, "g": g}
+    known = {q: {} for q in Q}
+    snap = {}
+    cnt = {q: 0 for q in ENG}
+    hist = {}
+    allsem = {}
+    nd = [0]
+
+    def wait(q, tok):
+        sem, val = tok
+        if known[q].get(sem, 0) >= val:
+            return
+        Q[q].wait_ge(T.sem[sem], val)
+        known[q][sem] = val
+        for s2, v2 in snap.get(tok, {}).items():
+            known[q][s2] = max(known[q].get(s2, 0), v2)
+
+    def waits(q, q0, reads, writes):
+        toks = {}
+        for wr, accs in ((False, reads), (True, writes)):
+            for buf, lo, hi in accs:
+                for (l, h, w, q2, tok) in hist.get(buf, ()):
+                    same = q2 == q0 and q0 != "dma"
+                    if buf in PSUM and not same:
+                        hit = l // 512 <= (hi - 1) // 512 and lo // 512 <= (h - 1) // 512
+                    else:
+                        hit = l < hi and lo < h and (w or wr) and not (same and q0 == "t")
+                    if hit:
+                        toks[tok[0]] = max(toks.get(tok[0], 0), tok[1])
+        for s in sorted(toks):
+            wait(q, (s, toks[s]))
+
+    def note(q, reads, writes, tok):
+        for buf, lo, hi in writes:
+            hist[buf] = [e for e in hist.get(buf, ()) if not (lo <= e[0] and e[1] <= hi)] + [(lo, hi, True, q, tok)]
+        for buf, lo, hi in reads:
+            hist[buf] = [e for e in hist.get(buf, ()) if not (lo <= e[0] and e[1] <= hi and not e[2] and e[3] == q and q in ENG)] + [(lo, hi, False, q, tok)]
+
+    def R(n, a=0, b=None):
+        b = SCRATCH[n][1][-1] if b is None else b
+        return (T[n][:, a:b], [(n, a, b)])
+
+    def ind(win, off):
+        return (win[0].indirect(off[0]), win[1] + off[1])
+
+    def op(q, fn, ins, outs):
+        rd = [r for v in ins if isinstance(v, tuple) for r in v[1]]
+        wr = [r for v in outs for r in v[1]]
+        waits(q, q, rd, wr)
+        i = fn()
+        cnt[q] += 1
+        i.then_inc(T.sem[ENG[q]], 1)
+        tok = (ENG[q], cnt[q])
+        allsem[ENG[q]] = cnt[q]
+        snap[tok] = dict(known[q])
+        note(q, rd, wr, tok)
+
+    def dma(qs, items, ins, outs):
+        sem = DSEM[nd[0]]
+        nd[0] += 1
+        kn = {}
+        for q in qs:
+            waits(q, "dma", ins, outs)
+            for s, v in known[q].items():
+                kn[s] = max(kn.get(s, 0), v)
+        for j, (o, i) in enumerate(items):
+            Q[qs[j % len(qs)]].dma_start(o, i).then_inc(T.sem[sem], 16)
+        tok = (sem, 16 * len(items))
+        allsem[sem] = tok[1]
+        snap[tok] = kn
+        note("dma", ins, outs, tok)
+
+    sc_ = lambda v: v[0] if isinstance(v, tuple) else v
+
+    def tt(o, a, b, f):
+        op("v", lambda: g.vector.tensor_tensor(o[0], a[0], b[0], f), [a, b], [o])
+
+    def ts(o, a, f, s, f2=None, s2=None):
+        if f2 is None:
+            op("v", lambda: g.vector.tensor_scalar(o[0], a[0], sc_(s), None, f), [a, s], [o])
+        else:
+            op("v", lambda: g.vector.tensor_scalar(o[0], a[0], sc_(s), sc_(s2), f, f2), [a, s, s2], [o])
+
+    def cp(o, a):
+        op("v", lambda: g.vector.tensor_copy(o[0], a[0]), [a], [o])
+
+    def act(o, a, bias=0.0, scale=1.0):
+        op("s", lambda: g.scalar.activation(o[0], a[0], F.Identity, bias=sc_(bias), scale=scale), [a, bias], [o])
+
+    def fill(o, c):
+        op("v", lambda: g.vector.memset(o[0], c), [], [o])
+
+    def mm(o, calls, ins):
+        def fn():
+            last = None
+            for c in calls:
+                last = g.tensor.matmul(*c)
+            return last
+        op("t", fn, ins, [o])
+
+    others = [k for k in range(4) if k != me]
+    off = [k for k in others if topo.chip(T.cores[k]) != topo.chip(core)]
+    on = [k for k in others if k not in off]
+    eo = topo.engines(core, T.cores[off[0]])
+    el = [e for e in topo.engines(core, T.cores[on[0]]) if e not in eo]
+    eng = {}
+    for ks, es in ((off, eo), (on, el)):
+        n = len(es) // len(ks)
+        for j, k in enumerate(ks):
+            eng[k] = es[j * n:j * n + n]
+    ARR = len(eo) + len(el)
+    nloc = [0]
+
+    def send(sem, need, src, dst):
+        waits("g", "dma", [need], [])
+        tr = []
+        for k in others:
+            rid, pid, _se = topo.addr(T.cores[k])
+            tr.append(RemoteDMATransfer(dst_ids=[DstId(rid=rid, pnc=pid)], dma_engine_mask=sum(1 << e for e in eng[k]), remote_sem=T.sem[sem], src=src(k), dst=dst))
+            nloc[0] += len(eng[k])
+        g.remote_dma_fused(tr, local_sem=T.sem["r_loc"])
+
+    def rwait(buf, lo, hi, sem):
+        allsem[sem] = ARR
+        hist.setdefault(buf, []).append((lo, hi, True, "remote", (sem, ARR)))
+
+    SO = [(s, o) for s in range(2) for o in range(4)]
+    rows = lambda s, o: slice(64 * s + 16 * o, 64 * s + 16 * o + 16)
+    mine = lambda s: slice(32 * me + 16 * s, 32 * me + 16 * s + 16)
+    CG = [T.cg0, T.cg1, T.cg2]
+    own = slice(192 * me, 192 * me + 192)
+
+    def fetch(t, q):
+        dma(q, [(T.cr[:, :, t, :, m, :], T.cand[:, 768 * t + 256 * m:768 * t + 256 * m + 256]) for m in range(3)], [], [("cr", t, t + 1)])
+
+    def stage(t, qs):
+        dma(qs, [(T.sc[4 * t:4 * t + 4, rows(s, o), :], T.cr[:, 16 * s:16 * s + 16, t, o]) for s, o in SO], [("cr", t, t + 1)], [("sc", t, t + 1)])
+
+    dma("y", [(T.sr[:], T.ray[:])], [], [("sr", 0, 4)])
+    fetch(0, "s")
+    stage(0, "sy")
+    dma("s", [(T.cg0[:, own], T.sc[me])], [("sc", 0, 1)], [("cg0", 0, 768)])
+    dma("s", [(T.sp[:], T.px[:])], [], [("sp", 0, 4)])
+    dma("s", [(T.tho[:], T.th[:]), (T.thl[:, me:me + 1], T.th[:])], [], [("tho", 0, 1), ("thl", 0, 4)])
+    for n, w, pat, base, cm in (("it1", 143, [[1, 143]], -15, -1), ("it0", 143, [[1, 143]], 0, 0), ("pc", 1, [[0, 1]], 0, 1), ("vci", 384, [[0, 12], [16, 32]], -255, 0)):
+        op("g", lambda: g.iota(T[n][:, 0:w], pat, base, cm), [], [R(n)])
+    send("r_ray", ("sr", 0, 4), lambda k: T.sr[k], T.lr[me])
+    send("r_c0", ("sc", 0, 1), lambda k: T.sc[k], T.cg0[:, own])
+    send("r_px", ("sp", 0, 4), lambda k: T.sp[k], T.lp[me])
+    send("r_th", ("tho", 0, 1), lambda k: T.tho[:], T.thl[:, me:me + 1])
+    rwait("lr", 0, 4, "r_ray")
+    rwait("cg0", 0, 768, "r_c0")
+    rwait("lp", 0, 4, "r_px")
+    rwait("thl", 0, 4, "r_th")
+
+    ts(R("lane"), R("pc"), A.bitwise_and, 15)
+    ts(R("grp"), R("pc"), A.arith_shift_right, 4)
+    cp(R("lanef"), R("lane"))
+    ts(R("oi"), R("grp"), A.bitwise_and, 3)
+    cp(R("grpf"), R("grp"))
+    ts(R("k0"), R("lane"), A.is_equal, 0)
+    cp(R("of"), R("oi"))
+    ts(R("nk0"), R("k0"), A.mult, -1.0)
+    ts(R("g16"), R("grpf"), A.mult, 16.0, A.add, 15.0)
+    for h in range(2):
+        ts(R("nb", h, h + 1), R("of"), A.mult, -1024.0, A.add, -(512.0 * h + 255.0))
+        ts(R("pb", h, h + 1), R("of"), A.mult, 1024.0, A.add, 512.0 * h + 255.0)
+    ts(R("xi4"), R("it0", 4, 8), A.subtract, R("of"))
+    ts(R("cole"), R("of"), A.mult, -1024.0, A.add, 4096.0)
+    ts(R("xj4"), R("xi4"), A.bitwise_and, 3)
+    fill(R("wt"), 0.0)
+    ts(R("colx"), R("xj4"), A.mult, 2048.0)
+    ts(R("mcb", 0, 143), R("it1", 0, 143), A.is_equal, 0, A.mult, R("nk0"))
+    ts(R("mid"), R("it1", 15, 143), A.is_equal, 0)
+    ts(R("vct"), R("vci"), A.add, R("lanef"))
+    ts(R("mb2", 0, 143), R("it0", 0, 143), A.subtract, R("g16"), A.is_equal, 0.0)
+    ts(R("ish"), R("it1", 15, 143), A.arith_shift_right, 4)
+    ts(R("im16"), R("it0", 0, 128), A.arith_shift_right, 4)
+    ts(R("lmk"), R("it0", 0, 16), A.is_equal, R("lanef"))
+    ts(R("mgt"), R("it1", 15, 143), A.is_gt, 0)
+    ts(R("mbc"), R("ish"), A.is_equal, 0, A.mult, R("k0"))
+    ts(R("mbo"), R("im16"), A.is_equal, R("grpf"))
+    fill(R("mt"), 0.0)
+    tt(R("mtri"), R("mbo"), R("mgt"), A.mult)
+    for i in range(16):
+        ts(R("mex", 128 * i, 128 * i + 128), R("mbo"), A.mult, R("lmk", i, i + 1))
+    fill(R("et", 4096, 4104), 0.0)
+    fill(R("zz"), 0.0)
+    fill(R("cu", 0, 16), 0.0)
+    fill(R("cc"), 0.0)
+
+    dma("y", [(T.rayi[rows(s, a), :], T.ray[mine(s), :] if a == me else T.lr[a, 64 * s:64 * s + 64, :]) for s, a in SO], [("lr", 0, 4)], [("rayi", 0, 768)])
+    L = ["la", "lb"]
+
+    def place_lists(n):
+        cp(R("ln"), R(n, 0, 256))
+        ts(R("zi"), R(n, 0, 256), A.add, R("cole"))
+        ts(R("zi"), R("zi"), A.bitwise_and, 4095)
+        ts(R("zf"), R("zi"), A.add, -4096.0)
+
+    def table_w(n):
+        dma("y", [(T.wt[64 * s + 16 * a:64 * s + 16 * a + 1, :], T[n][64 * s:64 * s + 64, 0:128]) for s, a in SO], [(n, 0, 128)], [("wt", 0, 8192)])
+
+    def spread(n, lo, w, width):
+        items = []
+        b = T[n]
+        for d in (1, 2, 3):
+            c = d * width + lo
+            for p in (0, 64):
+                k = p + 16 * (4 - d)
+                items.append((b[p:k, c:c + w], b[p + 16 * d:p + 64, lo:lo + w]))
+                items.append((b[k:p + 64, c:c + w], b[p:p + 16 * d, lo:lo + w]))
+        dma("y", items, [(n, lo, lo + w)], [(n, d * width + lo, d * width + lo + w) for d in (1, 2, 3)])
+
+    def prep(t, b):
+        c, lw, p = R("cg%d" % t), "lw%d" % t, R(b, 0, 768)
+        ts(R("ca"), c, A.bitwise_and, 15)
+        ts(p, R("ca"), A.mult, 2047.0)
+        tt(p, c, p, A.add)
+        for a in range(4):
+            ts(R(lw, 192 * a, 192 * a + 192), R(b, 192 * a, 192 * a + 192), A.mult, 0.0625, A.add, 2048.0 * a)
+
+    def prepx(t):
+        for h in range(2):
+            for k in range(12):
+                c = 384 * h + 32 * k
+                ts(R("xb%d" % t, c, c + 32), R("cg%d" % t, 64 * k + 32 * h, 64 * k + 32 * h + 32), A.add, R("colx", k // 3, k // 3 + 1))
+
+    cp(R("la", 0, 128), R("rayi", 0, 128))
+    table_w("la")
+    cp(R("la", 128, 768), R("rayi", 128, 768))
+    place_lists("la")
+    prep(0, "pA")
+    dma("y", [(T.xi[rows(s, a), :], T.px[mine(s), :] if a == me else T.lp[a, 64 * s:64 * s + 64, :]) for s, a in SO], [("lp", 0, 4)], [("xi", 0, 2048)])
+
+    def look_w(t, h, ks, q):
+        for k in ks:
+            o = R("wr", 6144 * h + 512 * k, 6144 * h + 512 * k + 512)
+            src = ind(R("wt"), R("lw%d" % t, 64 * k + 32 * h, 64 * k + 32 * h + 32))
+            if q == "s":
+                act(o, src, bias=R("nb", h, h + 1))
+            else:
+                ts(o, src, A.subtract, R("pb", h, h + 1))
+
+    def list_form(h):
+        o, w0 = R("pB", 512 * h, 512 * h + 384), 6144 * h
+        mm(o, [(o[0], T.mid[:], T.vct[:], True, False)] + [(o[0], T.mcb[:, 15 - i:143 - i], T.wr[:, w0 + i:w0 + 6144:16], False, i == 15) for i in range(16)],
+           [R("mid"), R("vct"), R("mcb"), R("wr", w0, w0 + 6144)])
+
+    def lists(t, h):
+        p, E = R("pB", 512 * h, 512 * h + 384), R("le")
+        yield ts(p, p, A.max, 0.0, A.mult, 8192.0)
+        yield tt(E, R("xb%d" % t, 384 * h, 384 * h + 384), p, A.subtract)
+        yield tt(R("l1"), R("le", 0, 192), R("le", 192, 384), A.max)
+        yield tt(R("l2"), R("l1", 0, 96), R("l1", 96, 192), A.max)
+        yield tt(R("l3"), R("l2", 0, 32), R("l2", 32, 64), A.max)
+        tt(R("lm", 0, 32), R("l3"), R("l2", 64, 96), A.max)
+        yield tt(R("lm", 32, 64), R("l3"), R("l2", 64, 96), A.max)
+        yield cp(R("lm", 64, 128), R("lm", 0, 64))
+        cp(R("lm", 128, 256), R("lm", 0, 128))
+        yield cp(R("lm", 256, 384), R("lm", 0, 128))
+        yield tt(p, p, R("lm"), A.min)
+        yield tt(R("le2"), E, p, A.max)
+        yield cp(R("lx", 384 * h, 384 * h + 384), R("le2"))
+
+    def acc(h):
+        return R("pA", 1024 * h, 1024 * h + 512), R("pA", 1024 * h + 512, 1024 * h + 1024)
+
+    def gather_x(h, k):
+        j = 512 * ((12 * h + k) % 8)
+        G = R("xg", j, j + 512)
+        act(G, ind(R("xw"), R("lx", 384 * h + 32 * k, 384 * h + 32 * k + 32)))
+        if k == 0:
+            act(acc(h)[1], G)
+
+    def minmax(h, k):
+        j = 512 * ((12 * h + k) % 8)
+        G = R("xg", j, j + 512)
+        lo, hi = acc(h)
+        if k:
+            tt(R("et", 512 * h, 512 * h + 512) if k == 11 else lo, G, hi if k == 1 else lo, A.min)
+            tt(hi, G, hi, A.max)
+
+    def flags(h):
+        c = 512 * h
+        lt, fl = R("lt", c, c + 512), R("fl", c, c + 512)
+        act(lt, R("et", c, c + 512), bias=R("thf"))
+        tt(fl, acc(h)[1], lt, A.is_gt)
+        mm(R("pC", 0, 64), [(T.pC[:, 0:64], T.mb2[:, 15 - i:143 - i], T.fl[:, 64 * i:64 * i + 64], i == 0, i == 15) for i in range(8 * h, 8 * h + 8)], [fl, R("mb2")])
+
+    f1, f2 = R("f1"), R("pD", 0, 128)
+
+    def place(k, old, new):
+        c = 128 * k
+        tt(R("fu"), R("dd", c, c + 128), f1, A.mult)
+        tt(R("pD", 128, 256), R("dd", c + 128, c + 256), f2, A.mult)
+        tt(R("fu"), R("fu"), R(old, c, c + 128), A.add)
+        tt(R(new, c, c + 128), R("fu"), R("pD", 128, 256), A.add)
+
+    def cursors():
+        tt(R("cc"), R("cc"), f1, A.add)
+        tt(R("cc"), R("cc"), f2, A.add)
+
+    KEEP = (4, 2, 0)
+    for t in range(3):
+        last = t == 2
+        old, new = L[t % 2], L[1 - t % 2]
+        for h in range(2):
+            n = VSHARE[h]
+            look_w(t, h, range(0, 12 - n), "s")
+            if h == 0:
+                look_w(t, h, range(12 - n, 12), "v")
+                list_form(0)
+        if t == 0:
+            prepx(0)
+            cp(R("xw", 0, 1024), R("xi", 0, 1024))
+            cp(R("xw", 1024, 2048), R("xi", 1024, 2048))
+            spread("xw", 0, 2048, 2048)
+            dma("y", [(T.thi[rows(s, o), :], T.thl[mine(s), o:o + 1]) for s, o in SO], [("thl", 0, 4)], [("thi", 0, 1)])
+            for u in (1, 2):
+                fetch(u, "y")
+                stage(u, "y")
+                dma("y", [(CG[u][:, own], T.sc[4 * u + me])], [("sc", u, u + 1)], [("cg%d" % u, 0, 768)])
+                send("r_c%d" % u, ("sc", u, u + 1), lambda k: T.sc[4 * u + k], CG[u][:, own])
+                rwait("cg%d" % u, 0, 768, "r_c%d" % u)
+        else:
+            for k in range(1, KEEP[t - 1]):
+                place(k, new, old)
+            cursors()
+            place_lists(old)
+        for _ in lists(t, 0):
+            pass
+        look_w(t, 1, range(12 - VSHARE[1], 12), "v")
+        list_form(1)
+        gen = lists(t, 1)
+        for k in range(12):
+            gather_x(0, k)
+            minmax(0, k)
+            next(gen, None)
+        for _ in gen:
+            pass
+        if t == 0:
+            cp(R("thf"), R("thi"))
+        if not last:
+            w = 128 * (KEEP[t] + 1)
+            tt(R("dd", 0, w), R(old, 128, 128 + w), R(old, 0, w), A.subtract)
+        spread("et", 0, 512, 1024)
+        for k in range(12):
+            gather_x(1, k)
+            if k == 2:
+                flags(0)
+            minmax(1, k)
+        spread("et", 512, 512, 1024)
+        flags(1)
+        ts(R("odd"), R("pC", 0, 64), A.is_ge, 9.0)
+        op("v", lambda: g.vector.tensor_tensor_scan(T.cu[:, 16:80], T.odd[:], T.zz[:], 0.0, A.add, A.max), [R("odd"), R("zz")], [R("cu", 16, 80)])
+        mm(R("pD", 0, 1), [(T.pD[:, 0:1], T.mtri[:], T.cu[:, 79:80], True, True)], [R("cu", 16, 80), R("mtri")])
+        ts(R("cs", 15, 80), R("cu", 15, 80), A.add, R("pD", 0, 1), A.min, 256.0)
+        tt(R("cv"), R("cs", 16, 80), R("cs", 15, 79), A.subtract)
+        dma("ys", [(T.mt[64 * s + 16 * a:64 * s + 16 * a + 1, :], T.cv[64 * s:64 * s + 64, :]) for s, a in SO], [("cv", 0, 64)], [("mt", 0, 4096)])
+        if not last:
+            prep(t + 1, "pB")
+            prepx(t + 1)
+        for st in range(2):
+            pn = ("pC", "pD")[st]
+            f, z, fz, oe = (f1, f2)[st], R("zf", 128 * st, 128 * st + 128), R("ft", 128 * st, 128 * st + 128), R("oe", 128 * st, 128 * st + 128)
+            for c in range(2):
+                b, l0 = 2048 * st + 1024 * c, 128 * st + 64 * c
+                act(R("wr", b, b + 1024), ind(R("mt"), R("ln", l0, l0 + 64)), bias=1.0, scale=0.25)
+                o = R(pn, 64 * c, 64 * c + 64)
+                mm(o, [(o[0], T.mcb[:, 15 - i:143 - i], T.wr[:, b + i:b + 1024:16], i == 0, i == 15) for i in range(16)], [R("wr", b, b + 1024), R("mcb")])
+            if st == 0:
+                for b in range(0, 2048, 512):
+                    o = R("pA", b, b + 512)
+                    mm(o, [(o[0], T.mbc[:], T.wr[:, b:b + 512], True, True)], [R("wr", b, b + 512), R("mbc")])
+            ts(f, R(pn, 0, 128), A.mult, -4.0, A.add, -4.0)
+            if st:
+                tt(f2, f1, f2, A.mult)
+            tt(fz, z, f, A.mult)
+            if st:
+                ts(R("m2"), f2, A.mult, 0.25, A.add, 1.0)
+            ts(oe, fz, A.add, 4096.0)
+        ch = CHUNKS_END if last else CHUNKS
+        for x0, x1 in ch:
+            for b in (0, 2048):
+                act(R("eg", b + x0, b + x1), ind(R("et"), R("oe", (b + x0) // 16, (b + x1) // 16)), bias=-0.375, scale=-0.25)
+        if not last:
+            place(0, old, new)
+            table_w(new)
+        else:
+            cursors()
+            ts(R("cf"), R("cc"), A.min, 5.0)
+            dma("y", [(T.sy[a, 64 * s:64 * s + 64, :], T.cf[rows(s, a), :]) for s, a in SO if a != me], [("cf", 0, 128)], [("sy", 0, 4)])
+            dma("y", [(T.yc[mine(s), :], T.cf[rows(s, me), :]) for s in range(2)], [("cf", 0, 128)], [])
+            send("r_yc", ("sy", 0, 4), lambda k: T.sy[k], T.ly[me])
+            rwait("ly", 0, 4, "r_yc")
+        for x0, x1 in ch:
+            for st in range(2):
+                x, m, y = R("xw", x0, x1), R("pA", x0, x1), R("xi", x0, x1)
+                if st == 1:
+                    for b in range(x0 // 512, x1 // 512):
+                        mm(R("pA", 512 * b, 512 * b + 512), [(T.pA[:, 512 * b + i:512 * b + 512:16], T.mex[:, 128 * i:128 * i + 128], T.m2[:, 32 * b:32 * b + 32], True, True)
+                                                             for i in range(16)], [R("mex"), R("m2")])
+                tt(m, x, m, A.mult)
+                tt(y, R("eg", 2048 * st + x0, 2048 * st + x1), m, A.add)
+                ts(x, y, A.max, 0.0, A.min, float(TOP))
+            if not last:
+                spread("xw", x0, x1 - x0, 2048)
+            else:
+                c = x0 // 512
+                dma("ys", [(T.so[4 * c + a, 64 * s:64 * s + 64, :], T.xw[rows(s, a), x0:x1]) for s, a in SO if a != me], x[1], [("so", 4 * c, 4 * c + 4)])
+                dma("y", [(T.yx[mine(s), x0:x1], T.xw[rows(s, me), x0:x1]) for s in range(2)], x[1], [])
+                send("r_x%d" % c, ("so", 4 * c, 4 * c + 4), lambda k: T.so[4 * c + k], T.lo[4 * c + me])
+                rwait("lo", 4 * c, 4 * c + 4, "r_x%d" % c)
+
+    dma("y", [(T.yc[32 * k:32 * k + 32, :], T.ly[k]) for k in others], [("ly", 0, 4)], [])
+    for c in range(4):
+        dma("ys", [(T.yx[32 * k:32 * k + 32, 512 * c:512 * c + 512], T.lo[4 * c + k]) for k in others], [("lo", 4 * c, 4 * c + 4)], [])
+    g.wait_ge(T.sem["r_loc"], nloc[0])
+    for s in sorted(allsem):
+        wait("y", (s, allsem[s]))

@@ -24,8 +24,8 @@ PSUM = ("pA", "pB", "pC", "pD")
 ENG = {"v": "q_v", "s": "q_s", "t": "q_t", "g": "q_g"}
 DSEM = ["d%d" % j for j in range(64)]
 SEMAPHORES = list(ENG.values()) + DSEM + ["r_ray", "r_c0", "r_px", "r_th", "r_c1", "r_c2", "r_yc", "r_x0", "r_x1", "r_x2", "r_x3", "r_loc"]
-VSHARE = (0, 1)
-CHUNKS = ((0, 1024), (1024, 1536), (1536, 2048))
+VSHARE = 3
+CHUNKS = ((0, 1024), (1024, 2048))
 CHUNKS_END = ((0, 512), (512, 1024), (1024, 1536), (1536, 2048))
 
 
@@ -174,8 +174,8 @@ def rank_program(g, core, T, topo):
     dma("y", [(T.sr[:], T.ray[:])], [], [("sr", 0, 4)])
     fetch(0, "s")
     stage(0, "sy")
+    dma("y", [(T.sp[:], T.px[:])], [], [("sp", 0, 4)])
     dma("s", [(T.cg0[:, own], T.sc[me])], [("sc", 0, 1)], [("cg0", 0, 768)])
-    dma("s", [(T.sp[:], T.px[:])], [], [("sp", 0, 4)])
     dma("s", [(T.tho[:], T.th[:]), (T.thl[:, me:me + 1], T.th[:])], [], [("tho", 0, 1), ("thl", 0, 4)])
     for n, w, pat, base, cm in (("it1", 143, [[1, 143]], -15, -1), ("it0", 143, [[1, 143]], 0, 0), ("pc", 1, [[0, 1]], 0, 1), ("vci", 384, [[0, 12], [16, 32]], -255, 0)):
         op("g", lambda: g.iota(T[n][:, 0:w], pat, base, cm), [], [R(n)])
@@ -188,6 +188,7 @@ def rank_program(g, core, T, topo):
     rwait("lp", 0, 4, "r_px")
     rwait("thl", 0, 4, "r_th")
 
+    fill(R("wt"), 0.0)
     ts(R("lane"), R("pc"), A.bitwise_and, 15)
     ts(R("grp"), R("pc"), A.arith_shift_right, 4)
     cp(R("lanef"), R("lane"))
@@ -203,26 +204,10 @@ def rank_program(g, core, T, topo):
     ts(R("xi4"), R("it0", 4, 8), A.subtract, R("of"))
     ts(R("cole"), R("of"), A.mult, -1024.0, A.add, 4096.0)
     ts(R("xj4"), R("xi4"), A.bitwise_and, 3)
-    fill(R("wt"), 0.0)
     ts(R("colx"), R("xj4"), A.mult, 2048.0)
     ts(R("mcb", 0, 143), R("it1", 0, 143), A.is_equal, 0, A.mult, R("nk0"))
     ts(R("mid"), R("it1", 15, 143), A.is_equal, 0)
     ts(R("vct"), R("vci"), A.add, R("lanef"))
-    ts(R("mb2", 0, 143), R("it0", 0, 143), A.subtract, R("g16"), A.is_equal, 0.0)
-    ts(R("ish"), R("it1", 15, 143), A.arith_shift_right, 4)
-    ts(R("im16"), R("it0", 0, 128), A.arith_shift_right, 4)
-    ts(R("lmk"), R("it0", 0, 16), A.is_equal, R("lanef"))
-    ts(R("mgt"), R("it1", 15, 143), A.is_gt, 0)
-    ts(R("mbc"), R("ish"), A.is_equal, 0, A.mult, R("k0"))
-    ts(R("mbo"), R("im16"), A.is_equal, R("grpf"))
-    fill(R("mt"), 0.0)
-    tt(R("mtri"), R("mbo"), R("mgt"), A.mult)
-    for i in range(16):
-        ts(R("mex", 128 * i, 128 * i + 128), R("mbo"), A.mult, R("lmk", i, i + 1))
-    fill(R("et", 4096, 4104), 0.0)
-    fill(R("zz"), 0.0)
-    fill(R("cu", 0, 16), 0.0)
-    fill(R("cc"), 0.0)
 
     dma("y", [(T.rayi[rows(s, a), :], T.ray[mine(s), :] if a == me else T.lr[a, 64 * s:64 * s + 64, :]) for s, a in SO], [("lr", 0, 4)], [("rayi", 0, 768)])
     L = ["la", "lb"]
@@ -232,6 +217,25 @@ def rank_program(g, core, T, topo):
         ts(R("zi"), R(n, 0, 256), A.add, R("cole"))
         ts(R("zi"), R("zi"), A.bitwise_and, 4095)
         ts(R("zf"), R("zi"), A.add, -4096.0)
+
+    def consts():
+        ts(R("mb2", 0, 143), R("it0", 0, 143), A.subtract, R("g16"), A.is_equal, 0.0)
+        ts(R("ish"), R("it1", 15, 143), A.arith_shift_right, 4)
+        ts(R("im16"), R("it0", 0, 128), A.arith_shift_right, 4)
+        ts(R("lmk"), R("it0", 0, 16), A.is_equal, R("lanef"))
+        ts(R("mgt"), R("it1", 15, 143), A.is_gt, 0)
+        ts(R("mbc"), R("ish"), A.is_equal, 0, A.mult, R("k0"))
+        ts(R("mbo"), R("im16"), A.is_equal, R("grpf"))
+        fill(R("mt"), 0.0)
+        tt(R("mtri"), R("mbo"), R("mgt"), A.mult)
+        for i in range(16):
+            ts(R("mex", 128 * i, 128 * i + 128), R("mbo"), A.mult, R("lmk", i, i + 1))
+        fill(R("et", 4096, 4104), 0.0)
+        fill(R("zz"), 0.0)
+        fill(R("cu", 0, 16), 0.0)
+        fill(R("cc"), 0.0)
+        cp(R("la", 128, 768), R("rayi", 128, 768))
+        place_lists("la")
 
     def table_w(n):
         dma("y", [(T.wt[64 * s + 16 * a:64 * s + 16 * a + 1, :], T[n][64 * s:64 * s + 64, 0:128]) for s, a in SO], [(n, 0, 128)], [("wt", 0, 8192)])
@@ -263,8 +267,6 @@ def rank_program(g, core, T, topo):
 
     cp(R("la", 0, 128), R("rayi", 0, 128))
     table_w("la")
-    cp(R("la", 128, 768), R("rayi", 128, 768))
-    place_lists("la")
     prep(0, "pA")
     dma("y", [(T.xi[rows(s, a), :], T.px[mine(s), :] if a == me else T.lp[a, 64 * s:64 * s + 64, :]) for s, a in SO], [("lp", 0, 4)], [("xi", 0, 2048)])
 
@@ -277,10 +279,10 @@ def rank_program(g, core, T, topo):
             else:
                 ts(o, src, A.subtract, R("pb", h, h + 1))
 
-    def list_form(h):
-        o, w0 = R("pB", 512 * h, 512 * h + 384), 6144 * h
-        mm(o, [(o[0], T.mid[:], T.vct[:], True, False)] + [(o[0], T.mcb[:, 15 - i:143 - i], T.wr[:, w0 + i:w0 + 6144:16], False, i == 15) for i in range(16)],
-           [R("mid"), R("vct"), R("mcb"), R("wr", w0, w0 + 6144)])
+    def list_form(h, j):
+        o, w0 = R("pB", 512 * h + 96 * j, 512 * h + 96 * j + 96), 6144 * h + 1536 * j
+        mm(o, [(o[0], T.mid[:], T.vct[:, 0:96], True, False)] + [(o[0], T.mcb[:, 15 - i:143 - i], T.wr[:, w0 + i:w0 + 1536:16], False, i == 15) for i in range(16)],
+           [R("mid"), R("vct"), R("mcb"), R("wr", w0, w0 + 1536)])
 
     def lists(t, h):
         p, E = R("pB", 512 * h, 512 * h + 384), R("le")
@@ -336,21 +338,48 @@ def rank_program(g, core, T, topo):
         tt(R("cc"), R("cc"), f1, A.add)
         tt(R("cc"), R("cc"), f2, A.add)
 
+    def flag(st, c):
+        b, l0 = 2048 * st + 1024 * c, 128 * st + 64 * c
+        act(R("wr", b, b + 1024), ind(R("mt"), R("ln", l0, l0 + 64)), bias=1.0, scale=0.25)
+        o = R(("pC", "pD")[st], 64 * c, 64 * c + 64)
+        mm(o, [(o[0], T.mcb[:, 15 - i:143 - i], T.wr[:, b + i:b + 1024:16], i == 0, i == 15) for i in range(16)], [R("wr", b, b + 1024), R("mcb")])
+
+    def colour(st, x0, x1):
+        b = 2048 * st
+        act(R("eg", b + x0, b + x1), ind(R("et"), R("oe", (b + x0) // 16, (b + x1) // 16)), bias=-0.375, scale=-0.25)
+
+    def colour_list(st, f):
+        c = 128 * st
+        tt(R("ft", c, c + 128), R("zf", c, c + 128), f, A.mult)
+        ts(R("oe", c, c + 128), R("ft", c, c + 128), A.add, 4096.0)
+
+    def step(st, x0, x1):
+        x, m, y = R("xw", x0, x1), R("pA", x0, x1), R("xi", x0, x1)
+        if st == 1:
+            for b in range(x0 // 512, x1 // 512):
+                mm(R("pA", 512 * b, 512 * b + 512), [(T.pA[:, 512 * b + i:512 * b + 512:16], T.mex[:, 128 * i:128 * i + 128], T.m2[:, 32 * b:32 * b + 32], True, True)
+                                                     for i in range(16)], [R("mex"), R("m2")])
+            tt(m, x, m, A.mult)
+        tt(y, R("eg", 2048 * st + x0, 2048 * st + x1), m, A.add)
+        ts(x, y, A.max, 0.0, A.min, float(TOP))
+
     KEEP = (4, 2, 0)
     for t in range(3):
         last = t == 2
         old, new = L[t % 2], L[1 - t % 2]
+        late = [j for j in range(4) if 3 * j + 3 > 12 - VSHARE]
         for h in range(2):
-            n = VSHARE[h]
-            look_w(t, h, range(0, 12 - n), "s")
-            if h == 0:
-                look_w(t, h, range(12 - n, 12), "v")
-                list_form(0)
+            for j in range(4):
+                look_w(t, h, [k for k in range(3 * j, 3 * j + 3) if h == 0 or k < 12 - VSHARE], "s")
+                if h == 0 or j not in late:
+                    list_form(h, j)
         if t == 0:
             prepx(0)
+            consts()
             cp(R("xw", 0, 1024), R("xi", 0, 1024))
+            spread("xw", 0, 1024, 2048)
             cp(R("xw", 1024, 2048), R("xi", 1024, 2048))
-            spread("xw", 0, 2048, 2048)
+            spread("xw", 1024, 1024, 2048)
             dma("y", [(T.thi[rows(s, o), :], T.thl[mine(s), o:o + 1]) for s, o in SO], [("thl", 0, 4)], [("thi", 0, 1)])
             for u in (1, 2):
                 fetch(u, "y")
@@ -365,13 +394,16 @@ def rank_program(g, core, T, topo):
             place_lists(old)
         for _ in lists(t, 0):
             pass
-        look_w(t, 1, range(12 - VSHARE[1], 12), "v")
-        list_form(1)
+        look_w(t, 1, range(12 - VSHARE, 12), "v")
+        for j in late:
+            list_form(1, j)
         gen = lists(t, 1)
         for k in range(12):
             gather_x(0, k)
             minmax(0, k)
-            next(gen, None)
+            if k > 2:
+                next(gen, None)
+                next(gen, None)
         for _ in gen:
             pass
         if t == 0:
@@ -385,7 +417,6 @@ def rank_program(g, core, T, topo):
             if k == 2:
                 flags(0)
             minmax(1, k)
-        spread("et", 512, 512, 1024)
         flags(1)
         ts(R("odd"), R("pC", 0, 64), A.is_ge, 9.0)
         op("v", lambda: g.vector.tensor_tensor_scan(T.cu[:, 16:80], T.odd[:], T.zz[:], 0.0, A.add, A.max), [R("odd"), R("zz")], [R("cu", 16, 80)])
@@ -393,32 +424,29 @@ def rank_program(g, core, T, topo):
         ts(R("cs", 15, 80), R("cu", 15, 80), A.add, R("pD", 0, 1), A.min, 256.0)
         tt(R("cv"), R("cs", 16, 80), R("cs", 15, 79), A.subtract)
         dma("ys", [(T.mt[64 * s + 16 * a:64 * s + 16 * a + 1, :], T.cv[64 * s:64 * s + 64, :]) for s, a in SO], [("cv", 0, 64)], [("mt", 0, 4096)])
+        spread("et", 512, 512, 1024)
         if not last:
             prep(t + 1, "pB")
             prepx(t + 1)
-        for st in range(2):
-            pn = ("pC", "pD")[st]
-            f, z, fz, oe = (f1, f2)[st], R("zf", 128 * st, 128 * st + 128), R("ft", 128 * st, 128 * st + 128), R("oe", 128 * st, 128 * st + 128)
-            for c in range(2):
-                b, l0 = 2048 * st + 1024 * c, 128 * st + 64 * c
-                act(R("wr", b, b + 1024), ind(R("mt"), R("ln", l0, l0 + 64)), bias=1.0, scale=0.25)
-                o = R(pn, 64 * c, 64 * c + 64)
-                mm(o, [(o[0], T.mcb[:, 15 - i:143 - i], T.wr[:, b + i:b + 1024:16], i == 0, i == 15) for i in range(16)], [R("wr", b, b + 1024), R("mcb")])
-            if st == 0:
-                for b in range(0, 2048, 512):
-                    o = R("pA", b, b + 512)
-                    mm(o, [(o[0], T.mbc[:], T.wr[:, b:b + 512], True, True)], [R("wr", b, b + 512), R("mbc")])
-            ts(f, R(pn, 0, 128), A.mult, -4.0, A.add, -4.0)
-            if st:
-                tt(f2, f1, f2, A.mult)
-            tt(fz, z, f, A.mult)
-            if st:
-                ts(R("m2"), f2, A.mult, 0.25, A.add, 1.0)
-            ts(oe, fz, A.add, 4096.0)
         ch = CHUNKS_END if last else CHUNKS
+        flag(0, 0)
+        flag(0, 1)
+        for b in range(0, 2048, 512):
+            o = R("pA", b, b + 512)
+            mm(o, [(o[0], T.mbc[:], T.wr[:, b:b + 512], True, True)], [R("wr", b, b + 512), R("mbc")])
+        flag(1, 0)
+        flag(1, 1)
+        ts(f1, R("pC", 0, 128), A.mult, -4.0, A.add, -4.0)
+        colour_list(0, f1)
         for x0, x1 in ch:
-            for b in (0, 2048):
-                act(R("eg", b + x0, b + x1), ind(R("et"), R("oe", (b + x0) // 16, (b + x1) // 16)), bias=-0.375, scale=-0.25)
+            tt(R("pA", x0, x1), R("xw", x0, x1), R("pA", x0, x1), A.mult)
+        ts(f2, f2, A.mult, -4.0, A.add, -4.0)
+        tt(f2, f1, f2, A.mult)
+        colour_list(1, f2)
+        ts(R("m2"), f2, A.mult, 0.25, A.add, 1.0)
+        for c in ch:
+            colour(0, *c)
+            colour(1, *c)
         if not last:
             place(0, old, new)
             table_w(new)
@@ -430,21 +458,14 @@ def rank_program(g, core, T, topo):
             send("r_yc", ("sy", 0, 4), lambda k: T.sy[k], T.ly[me])
             rwait("ly", 0, 4, "r_yc")
         for x0, x1 in ch:
-            for st in range(2):
-                x, m, y = R("xw", x0, x1), R("pA", x0, x1), R("xi", x0, x1)
-                if st == 1:
-                    for b in range(x0 // 512, x1 // 512):
-                        mm(R("pA", 512 * b, 512 * b + 512), [(T.pA[:, 512 * b + i:512 * b + 512:16], T.mex[:, 128 * i:128 * i + 128], T.m2[:, 32 * b:32 * b + 32], True, True)
-                                                             for i in range(16)], [R("mex"), R("m2")])
-                tt(m, x, m, A.mult)
-                tt(y, R("eg", 2048 * st + x0, 2048 * st + x1), m, A.add)
-                ts(x, y, A.max, 0.0, A.min, float(TOP))
+            step(0, x0, x1)
+            step(1, x0, x1)
             if not last:
                 spread("xw", x0, x1 - x0, 2048)
             else:
-                c = x0 // 512
-                dma("ys", [(T.so[4 * c + a, 64 * s:64 * s + 64, :], T.xw[rows(s, a), x0:x1]) for s, a in SO if a != me], x[1], [("so", 4 * c, 4 * c + 4)])
-                dma("y", [(T.yx[mine(s), x0:x1], T.xw[rows(s, me), x0:x1]) for s in range(2)], x[1], [])
+                c, x = x0 // 512, [("xw", x0, x1)]
+                dma("ys", [(T.so[4 * c + a, 64 * s:64 * s + 64, :], T.xw[rows(s, a), x0:x1]) for s, a in SO if a != me], x, [("so", 4 * c, 4 * c + 4)])
+                dma("y", [(T.yx[mine(s), x0:x1], T.xw[rows(s, me), x0:x1]) for s in range(2)], x, [])
                 send("r_x%d" % c, ("so", 4 * c, 4 * c + 4), lambda k: T.so[4 * c + k], T.lo[4 * c + me])
                 rwait("lo", 4 * c, 4 * c + 4, "r_x%d" % c)
 

from concourse.bass import DstId, RemoteDMATransfer
from concourse.mybir import AluOpType as A, ActivationFunctionType as F

TOP = 2 ** 20 - 1
SCRATCH = {}


def _buf(where, dtype, **shapes):
    for n, s in shapes.items():
        SCRATCH[n] = (where, s if isinstance(s, list) else [128, s], dtype)


_buf("dram", "int32", sp=[4, 128, 512], lp=[4, 128, 512], sr=[4, 128, 192], lr=[4, 128, 192], cr=[4, 32, 3, 4, 3, 64], sc=[12, 128, 192])
_buf("dram", "float32", so=[16, 128, 128], lo=[16, 128, 128], sy=[4, 128, 32], ly=[4, 128, 32])
_buf("sbuf", "int32", cg0=768, cg1=768, cg2=768, ca=768, xi=2048, rayi=768, tho=1, thl=4, thi=1,
     zi=256, it0=144, it1=144, vci=384, pc=1, lane=1, grp=1, oi=1, xi4=4, xj4=4, ish=128, im16=128)
_buf("sbuf", "uint16", lw0=768, lw1=768, lw2=768, lx=768, ln=256, oe=256)
_buf("sbuf", "bfloat16", wr=12288, fl=1024, m2=128, mcb=144, mid=128, mb2=144, mbc=128, mex=2048, vct=384)
_buf("sbuf", "float32", xb0=768, xb1=768, xb2=768, thf=1, xw=8192, wt=8192, mt=4096, et=4104, xg=4096, le=384, l1=192, l2=96,
     l3=32, lm=384, le2=384, lt=1024, odd=64, zz=64, cu=80, cs=80, cv=64, eg=4096, la=768, lb=768, dd=640, zf=256, f1=128, ft=256, fu=128,
     cc=128, cf=128, lanef=1, grpf=1, of=1, k0=1, nk0=1, g16=1, nb=2, pb=2, colx=4, cole=1, lmk=16, mbo=128, mgt=128, mtri=128)
_buf("psum", "float32", pA=2048, pB=1024, pC=512, pD=512)
PSUM = ("pA", "pB", "pC", "pD")
ENG = {"v": "q_v", "s": "q_s", "t": "q_t", "g": "q_g"}
DSEM = ["d%d" % j for j in range(64)]
SEMAPHORES = list(ENG.values()) + DSEM + ["r_ray", "r_c0", "r_px", "r_th", "r_c1", "r_c2", "r_yc", "r_x0", "r_x1", "r_x2", "r_x3", "r_loc"]
VSHARE = 3
CHUNKS = ((0, 1024), (1024, 2048))
CHUNKS_END = ((0, 512), (512, 1024), (1024, 1536), (1536, 2048))


def rank_program(g, core, T, topo):
    me = T.rank_of(core)
    if me is None:
        return
    Q = {"v": g.vector, "s": g.scalar, "t": g.tensor, "y": g.sync, "g": g}
    known = {q: {} for q in Q}
    snap = {}
    cnt = {q: 0 for q in ENG}
    hist = {}
    allsem = {}
    nd = [0]

    def wait(q, tok):
        sem, val = tok
        if known[q].get(sem, 0) >= val:
            return
        Q[q].wait_ge(T.sem[sem], val)
        known[q][sem] = val
        for s2, v2 in snap.get(tok, {}).items():
            known[q][s2] = max(known[q].get(s2, 0), v2)

    def waits(q, q0, reads, writes):
        toks = {}
        for wr, accs in ((False, reads), (True, writes)):
            for buf, lo, hi in accs:
                for (l, h, w, q2, tok) in hist.get(buf, ()):
                    same = q2 == q0 and q0 != "dma"
                    if buf in PSUM and not same:
                        hit = l // 512 <= (hi - 1) // 512 and lo // 512 <= (h - 1) // 512
                    else:
                        hit = l < hi and lo < h and (w or wr) and not (same and q0 == "t")
                    if hit:
                        toks[tok[0]] = max(toks.get(tok[0], 0), tok[1])
        for s in sorted(toks):
            wait(q, (s, toks[s]))

    def note(q, reads, writes, tok):
        for buf, lo, hi in writes:
            hist[buf] = [e for e in hist.get(buf, ()) if not (lo <= e[0] and e[1] <= hi)] + [(lo, hi, True, q, tok)]
        for buf, lo, hi in reads:
            hist[buf] = [e for e in hist.get(buf, ()) if not (lo <= e[0] and e[1] <= hi and not e[2] and e[3] == q and q in ENG)] + [(lo, hi, False, q, tok)]

    def R(n, a=0, b=None):
        b = SCRATCH[n][1][-1] if b is None else b
        return (T[n][:, a:b], [(n, a, b)])

    def ind(win, off):
        return (win[0].indirect(off[0]), win[1] + off[1])

    def op(q, fn, ins, outs):
        rd = [r for v in ins if isinstance(v, tuple) for r in v[1]]
        wr = [r for v in outs for r in v[1]]
        waits(q, q, rd, wr)
        i = fn()
        cnt[q] += 1
        i.then_inc(T.sem[ENG[q]], 1)
        tok = (ENG[q], cnt[q])
        allsem[ENG[q]] = cnt[q]
        snap[tok] = dict(known[q])
        note(q, rd, wr, tok)

    def dma(qs, items, ins, outs):
        sem = DSEM[nd[0]]
        nd[0] += 1
        kn = {}
        for q in qs:
            waits(q, "dma", ins, outs)
            for s, v in known[q].items():
                kn[s] = max(kn.get(s, 0), v)
        for j, (o, i) in enumerate(items):
            Q[qs[j % len(qs)]].dma_start(o, i).then_inc(T.sem[sem], 16)
        tok = (sem, 16 * len(items))
        allsem[sem] = tok[1]
        snap[tok] = kn
        note("dma", ins, outs, tok)

    sc_ = lambda v: v[0] if isinstance(v, tuple) else v

    def tt(o, a, b, f):
        op("v", lambda: g.vector.tensor_tensor(o[0], a[0], b[0], f), [a, b], [o])

    def ts(o, a, f, s, f2=None, s2=None):
        if f2 is None:
            op("v", lambda: g.vector.tensor_scalar(o[0], a[0], sc_(s), None, f), [a, s], [o])
        else:
            op("v", lambda: g.vector.tensor_scalar(o[0], a[0], sc_(s), sc_(s2), f, f2), [a, s, s2], [o])

    def cp(o, a):
        op("v", lambda: g.vector.tensor_copy(o[0], a[0]), [a], [o])

    def act(o, a, bias=0.0, scale=1.0):
        op("s", lambda: g.scalar.activation(o[0], a[0], F.Identity, bias=sc_(bias), scale=scale), [a, bias], [o])

    def fill(o, c):
        op("v", lambda: g.vector.memset(o[0], c), [], [o])

    def mm(o, calls, ins):
        def fn():
            last = None
            for c in calls:
                last = g.tensor.matmul(*c)
            return last
        op("t", fn, ins, [o])

    others = [k for k in range(4) if k != me]
    off = [k for k in others if topo.chip(T.cores[k]) != topo.chip(core)]
    on = [k for k in others if k not in off]
    eo = topo.engines(core, T.cores[off[0]])
    el = [e for e in topo.engines(core, T.cores[on[0]]) if e not in eo]
    eng = {}
    for ks, es in ((off, eo), (on, el)):
        n = len(es) // len(ks)
        for j, k in enumerate(ks):
            eng[k] = es[j * n:j * n + n]
    ARR = len(eo) + len(el)
    nloc = [0]

    def send(sem, need, src, dst):
        waits("g", "dma", [need], [])
        tr = []
        for k in others:
            rid, pid, _se = topo.addr(T.cores[k])
            tr.append(RemoteDMATransfer(dst_ids=[DstId(rid=rid, pnc=pid)], dma_engine_mask=sum(1 << e for e in eng[k]), remote_sem=T.sem[sem], src=src(k), dst=dst))
            nloc[0] += len(eng[k])
        g.remote_dma_fused(tr, local_sem=T.sem["r_loc"])

    def rwait(buf, lo, hi, sem):
        allsem[sem] = ARR
        hist.setdefault(buf, []).append((lo, hi, True, "remote", (sem, ARR)))

    SO = [(s, o) for s in range(2) for o in range(4)]
    rows = lambda s, o: slice(64 * s + 16 * o, 64 * s + 16 * o + 16)
    mine = lambda s: slice(32 * me + 16 * s, 32 * me + 16 * s + 16)
    CG = [T.cg0, T.cg1, T.cg2]
    own = slice(192 * me, 192 * me + 192)

    def fetch(t, q):
        dma(q, [(T.cr[:, :, t, :, m, :], T.cand[:, 768 * t + 256 * m:768 * t + 256 * m + 256]) for m in range(3)], [], [("cr", t, t + 1)])

    def stage(t, qs):
        dma(qs, [(T.sc[4 * t:4 * t + 4, rows(s, o), :], T.cr[:, 16 * s:16 * s + 16, t, o]) for s, o in SO], [("cr", t, t + 1)], [("sc", t, t + 1)])

    dma("y", [(T.sr[:], T.ray[:])], [], [("sr", 0, 4)])
    fetch(0, "s")
    stage(0, "sy")
    dma("y", [(T.sp[:], T.px[:])], [], [("sp", 0, 4)])
    dma("s", [(T.cg0[:, own], T.sc[me])], [("sc", 0, 1)], [("cg0", 0, 768)])
    dma("s", [(T.tho[:], T.th[:]), (T.thl[:, me:me + 1], T.th[:])], [], [("tho", 0, 1), ("thl", 0, 4)])
    for n, w, pat, base, cm in (("it1", 143, [[1, 143]], -15, -1), ("it0", 143, [[1, 143]], 0, 0), ("pc", 1, [[0, 1]], 0, 1), ("vci", 384, [[0, 12], [16, 32]], -255, 0)):
        op("g", lambda: g.iota(T[n][:, 0:w], pat, base, cm), [], [R(n)])
    send("r_ray", ("sr", 0, 4), lambda k: T.sr[k], T.lr[me])
    send("r_c0", ("sc", 0, 1), lambda k: T.sc[k], T.cg0[:, own])
    send("r_px", ("sp", 0, 4), lambda k: T.sp[k], T.lp[me])
    send("r_th", ("tho", 0, 1), lambda k: T.tho[:], T.thl[:, me:me + 1])
    rwait("lr", 0, 4, "r_ray")
    rwait("cg0", 0, 768, "r_c0")
    rwait("lp", 0, 4, "r_px")
    rwait("thl", 0, 4, "r_th")

    fill(R("wt"), 0.0)
    ts(R("lane"), R("pc"), A.bitwise_and, 15)
    ts(R("grp"), R("pc"), A.arith_shift_right, 4)
    cp(R("lanef"), R("lane"))
    ts(R("oi"), R("grp"), A.bitwise_and, 3)
    cp(R("grpf"), R("grp"))
    ts(R("k0"), R("lane"), A.is_equal, 0)
    cp(R("of"), R("oi"))
    ts(R("nk0"), R("k0"), A.mult, -1.0)
    ts(R("g16"), R("grpf"), A.mult, 16.0, A.add, 15.0)
    for h in range(2):
        ts(R("nb", h, h + 1), R("of"), A.mult, -1024.0, A.add, -(512.0 * h + 255.0))
        ts(R("pb", h, h + 1), R("of"), A.mult, 1024.0, A.add, 512.0 * h + 255.0)
    ts(R("xi4"), R("it0", 4, 8), A.subtract, R("of"))
    ts(R("cole"), R("of"), A.mult, -1024.0, A.add, 4096.0)
    ts(R("xj4"), R("xi4"), A.bitwise_and, 3)
    ts(R("colx"), R("xj4"), A.mult, 2048.0)
    ts(R("mcb", 0, 143), R("it1", 0, 143), A.is_equal, 0, A.mult, R("nk0"))
    ts(R("mid"), R("it1", 15, 143), A.is_equal, 0)
    ts(R("vct"), R("vci"), A.add, R("lanef"))

    dma("y", [(T.rayi[rows(s, a), :], T.ray[mine(s), :] if a == me else T.lr[a, 64 * s:64 * s + 64, :]) for s, a in SO], [("lr", 0, 4)], [("rayi", 0, 768)])
    L = ["la", "lb"]

    def place_lists(n):
        cp(R("ln"), R(n, 0, 256))
        ts(R("zi"), R(n, 0, 256), A.add, R("cole"))
        ts(R("zi"), R("zi"), A.bitwise_and, 4095)
        ts(R("zf"), R("zi"), A.add, -4096.0)

    def consts():
        ts(R("mb2", 0, 143), R("it0", 0, 143), A.subtract, R("g16"), A.is_equal, 0.0)
        ts(R("ish"), R("it1", 15, 143), A.arith_shift_right, 4)
        ts(R("im16"), R("it0", 0, 128), A.arith_shift_right, 4)
        ts(R("lmk"), R("it0", 0, 16), A.is_equal, R("lanef"))
        ts(R("mgt"), R("it1", 15, 143), A.is_gt, 0)
        ts(R("mbc"), R("ish"), A.is_equal, 0, A.mult, R("k0"))
        ts(R("mbo"), R("im16"), A.is_equal, R("grpf"))
        fill(R("mt"), 0.0)
        tt(R("mtri"), R("mbo"), R("mgt"), A.mult)
        for i in range(16):
            ts(R("mex", 128 * i, 128 * i + 128), R("mbo"), A.mult, R("lmk", i, i + 1))
        fill(R("et", 4096, 4104), 0.0)
        fill(R("zz"), 0.0)
        fill(R("cu", 0, 16), 0.0)
        fill(R("cc"), 0.0)
        cp(R("la", 128, 768), R("rayi", 128, 768))
        place_lists("la")

    def table_w(n):
        dma("y", [(T.wt[64 * s + 16 * a:64 * s + 16 * a + 1, :], T[n][64 * s:64 * s + 64, 0:128]) for s, a in SO], [(n, 0, 128)], [("wt", 0, 8192)])

    def spread(n, lo, w, width):
        items = []
        b = T[n]
        for d in (1, 2, 3):
            c = d * width + lo
            for p in (0, 64):
                k = p + 16 * (4 - d)
                items.append((b[p:k, c:c + w], b[p + 16 * d:p + 64, lo:lo + w]))
                items.append((b[k:p + 64, c:c + w], b[p:p + 16 * d, lo:lo + w]))
        dma("y", items, [(n, lo, lo + w)], [(n, d * width + lo, d * width + lo + w) for d in (1, 2, 3)])

    def prep(t, b):
        c, lw, p = R("cg%d" % t), "lw%d" % t, R(b, 0, 768)
        ts(R("ca"), c, A.bitwise_and, 15)
        ts(p, R("ca"), A.mult, 2047.0)
        tt(p, c, p, A.add)
        for a in range(4):
            ts(R(lw, 192 * a, 192 * a + 192), R(b, 192 * a, 192 * a + 192), A.mult, 0.0625, A.add, 2048.0 * a)

    def prepx(t):
        for h in range(2):
            for k in range(12):
                c = 384 * h + 32 * k
                ts(R("xb%d" % t, c, c + 32), R("cg%d" % t, 64 * k + 32 * h, 64 * k + 32 * h + 32), A.add, R("colx", k // 3, k // 3 + 1))

    cp(R("la", 0, 128), R("rayi", 0, 128))
    table_w("la")
    prep(0, "pA")
    dma("y", [(T.xi[rows(s, a), :], T.px[mine(s), :] if a == me else T.lp[a, 64 * s:64 * s + 64, :]) for s, a in SO], [("lp", 0, 4)], [("xi", 0, 2048)])

    def look_w(t, h, ks, q):
        for k in ks:
            o = R("wr", 6144 * h + 512 * k, 6144 * h + 512 * k + 512)
            src = ind(R("wt"), R("lw%d" % t, 64 * k + 32 * h, 64 * k + 32 * h + 32))
            if q == "s":
                act(o, src, bias=R("nb", h, h + 1))
            else:
                ts(o, src, A.subtract, R("pb", h, h + 1))

    def list_form(h, j):
        o, w0 = R("pB", 512 * h + 96 * j, 512 * h + 96 * j + 96), 6144 * h + 1536 * j
        mm(o, [(o[0], T.mid[:], T.vct[:, 0:96], True, False)] + [(o[0], T.mcb[:, 15 - i:143 - i], T.wr[:, w0 + i:w0 + 1536:16], False, i == 15) for i in range(16)],
           [R("mid"), R("vct"), R("mcb"), R("wr", w0, w0 + 1536)])

    def lists(t, h):
        p, E = R("pB", 512 * h, 512 * h + 384), R("le")
        yield ts(p, p, A.max, 0.0, A.mult, 8192.0)
        yield tt(E, R("xb%d" % t, 384 * h, 384 * h + 384), p, A.subtract)
        yield tt(R("l1"), R("le", 0, 192), R("le", 192, 384), A.max)
        yield tt(R("l2"), R("l1", 0, 96), R("l1", 96, 192), A.max)
        yield tt(R("l3"), R("l2", 0, 32), R("l2", 32, 64), A.max)
        tt(R("lm", 0, 32), R("l3"), R("l2", 64, 96), A.max)
        yield tt(R("lm", 32, 64), R("l3"), R("l2", 64, 96), A.max)
        yield cp(R("lm", 64, 128), R("lm", 0, 64))
        cp(R("lm", 128, 256), R("lm", 0, 128))
        yield cp(R("lm", 256, 384), R("lm", 0, 128))
        yield tt(p, p, R("lm"), A.min)
        yield tt(R("le2"), E, p, A.max)
        yield cp(R("lx", 384 * h, 384 * h + 384), R("le2"))

    def acc(h):
        return R("pA", 1024 * h, 1024 * h + 512), R("pA", 1024 * h + 512, 1024 * h + 1024)

    def gather_x(h, k):
        j = 512 * ((12 * h + k) % 8)
        G = R("xg", j, j + 512)
        act(G, ind(R("xw"), R("lx", 384 * h + 32 * k, 384 * h + 32 * k + 32)))
        if k == 0:
            act(acc(h)[1], G)

    def minmax(h, k):
        j = 512 * ((12 * h + k) % 8)
        G = R("xg", j, j + 512)
        lo, hi = acc(h)
        if k:
            tt(R("et", 512 * h, 512 * h + 512) if k == 11 else lo, G, hi if k == 1 else lo, A.min)
            tt(hi, G, hi, A.max)

    def flags(h):
        c = 512 * h
        lt, fl = R("lt", c, c + 512), R("fl", c, c + 512)
        act(lt, R("et", c, c + 512), bias=R("thf"))
        tt(fl, acc(h)[1], lt, A.is_gt)
        mm(R("pC", 0, 64), [(T.pC[:, 0:64], T.mb2[:, 15 - i:143 - i], T.fl[:, 64 * i:64 * i + 64], i == 0, i == 15) for i in range(8 * h, 8 * h + 8)], [fl, R("mb2")])

    f1, f2 = R("f1"), R("pD", 0, 128)

    def place(k, old, new):
        c = 128 * k
        tt(R("fu"), R("dd", c, c + 128), f1, A.mult)
        tt(R("pD", 128, 256), R("dd", c + 128, c + 256), f2, A.mult)
        tt(R("fu"), R("fu"), R(old, c, c + 128), A.add)
        tt(R(new, c, c + 128), R("fu"), R("pD", 128, 256), A.add)

    def cursors():
        tt(R("cc"), R("cc"), f1, A.add)
        tt(R("cc"), R("cc"), f2, A.add)

    def flag(st, c):
        b, l0 = 2048 * st + 1024 * c, 128 * st + 64 * c
        act(R("wr", b, b + 1024), ind(R("mt"), R("ln", l0, l0 + 64)), bias=1.0, scale=0.25)
        o = R(("pC", "pD")[st], 64 * c, 64 * c + 64)
        mm(o, [(o[0], T.mcb[:, 15 - i:143 - i], T.wr[:, b + i:b + 1024:16], i == 0, i == 15) for i in range(16)], [R("wr", b, b + 1024), R("mcb")])

    def colour(st, x0, x1):
        b = 2048 * st
        act(R("eg", b + x0, b + x1), ind(R("et"), R("oe", (b + x0) // 16, (b + x1) // 16)), bias=-0.375, scale=-0.25)

    def colour_list(st, f):
        c = 128 * st
        tt(R("ft", c, c + 128), R("zf", c, c + 128), f, A.mult)
        ts(R("oe", c, c + 128), R("ft", c, c + 128), A.add, 4096.0)

    def step(st, x0, x1):
        x, m, y = R("xw", x0, x1), R("pA", x0, x1), R("xi", x0, x1)
        if st == 1:
            for b in range(x0 // 512, x1 // 512):
                mm(R("pA", 512 * b, 512 * b + 512), [(T.pA[:, 512 * b + i:512 * b + 512:16], T.mex[:, 128 * i:128 * i + 128], T.m2[:, 32 * b:32 * b + 32], True, True)
                                                     for i in range(16)], [R("mex"), R("m2")])
            tt(m, x, m, A.mult)
        tt(y, R("eg", 2048 * st + x0, 2048 * st + x1), m, A.add)
        ts(x, y, A.max, 0.0, A.min, float(TOP))

    KEEP = (4, 2, 0)
    for t in range(3):
        last = t == 2
        old, new = L[t % 2], L[1 - t % 2]
        late = [j for j in range(4) if 3 * j + 3 > 12 - VSHARE]
        for h in range(2):
            for j in range(4):
                look_w(t, h, [k for k in range(3 * j, 3 * j + 3) if h == 0 or k < 12 - VSHARE], "s")
                if h == 0 or j not in late:
                    list_form(h, j)
        if t == 0:
            prepx(0)
            consts()
            cp(R("xw", 0, 1024), R("xi", 0, 1024))
            spread("xw", 0, 1024, 2048)
            cp(R("xw", 1024, 2048), R("xi", 1024, 2048))
            spread("xw", 1024, 1024, 2048)
            dma("y", [(T.thi[rows(s, o), :], T.thl[mine(s), o:o + 1]) for s, o in SO], [("thl", 0, 4)], [("thi", 0, 1)])
            for u in (1, 2):
                fetch(u, "y")
                stage(u, "y")
                dma("y", [(CG[u][:, own], T.sc[4 * u + me])], [("sc", u, u + 1)], [("cg%d" % u, 0, 768)])
                send("r_c%d" % u, ("sc", u, u + 1), lambda k: T.sc[4 * u + k], CG[u][:, own])
                rwait("cg%d" % u, 0, 768, "r_c%d" % u)
        else:
            for k in range(1, KEEP[t - 1]):
                place(k, new, old)
            cursors()
            place_lists(old)
        for _ in lists(t, 0):
            pass
        look_w(t, 1, range(12 - VSHARE, 12), "v")
        for j in late:
            list_form(1, j)
        gen = lists(t, 1)
        for k in range(12):
            gather_x(0, k)
            minmax(0, k)
            if k > 2:
                next(gen, None)
                next(gen, None)
        for _ in gen:
            pass
        if t == 0:
            cp(R("thf"), R("thi"))
        if not last:
            w = 128 * (KEEP[t] + 1)
            tt(R("dd", 0, w), R(old, 128, 128 + w), R(old, 0, w), A.subtract)
        spread("et", 0, 512, 1024)
        for k in range(12):
            gather_x(1, k)
            if k == 2:
                flags(0)
            minmax(1, k)
        flags(1)
        ts(R("odd"), R("pC", 0, 64), A.is_ge, 9.0)
        op("v", lambda: g.vector.tensor_tensor_scan(T.cu[:, 16:80], T.odd[:], T.zz[:], 0.0, A.add, A.max), [R("odd"), R("zz")], [R("cu", 16, 80)])
        mm(R("pD", 0, 1), [(T.pD[:, 0:1], T.mtri[:], T.cu[:, 79:80], True, True)], [R("cu", 16, 80), R("mtri")])
        ts(R("cs", 15, 80), R("cu", 15, 80), A.add, R("pD", 0, 1), A.min, 256.0)
        tt(R("cv"), R("cs", 16, 80), R("cs", 15, 79), A.subtract)
        dma("ys", [(T.mt[64 * s + 16 * a:64 * s + 16 * a + 1, :], T.cv[64 * s:64 * s + 64, :]) for s, a in SO], [("cv", 0, 64)], [("mt", 0, 4096)])
        spread("et", 512, 512, 1024)
        if not last:
            prep(t + 1, "pB")
            prepx(t + 1)
        ch = CHUNKS_END if last else CHUNKS
        flag(0, 0)
        flag(0, 1)
        for b in range(0, 2048, 512):
            o = R("pA", b, b + 512)
            mm(o, [(o[0], T.mbc[:], T.wr[:, b:b + 512], True, True)], [R("wr", b, b + 512), R("mbc")])
        flag(1, 0)
        flag(1, 1)
        ts(f1, R("pC", 0, 128), A.mult, -4.0, A.add, -4.0)
        colour_list(0, f1)
        for x0, x1 in ch:
            tt(R("pA", x0, x1), R("xw", x0, x1), R("pA", x0, x1), A.mult)
        ts(f2, f2, A.mult, -4.0, A.add, -4.0)
        tt(f2, f1, f2, A.mult)
        colour_list(1, f2)
        ts(R("m2"), f2, A.mult, 0.25, A.add, 1.0)
        for c in ch:
            colour(0, *c)
            colour(1, *c)
        if not last:
            place(0, old, new)
            table_w(new)
        else:
            cursors()
            ts(R("cf"), R("cc"), A.min, 5.0)
            dma("y", [(T.sy[a, 64 * s:64 * s + 64, :], T.cf[rows(s, a), :]) for s, a in SO if a != me], [("cf", 0, 128)], [("sy", 0, 4)])
            dma("y", [(T.yc[mine(s), :], T.cf[rows(s, me), :]) for s in range(2)], [("cf", 0, 128)], [])
            send("r_yc", ("sy", 0, 4), lambda k: T.sy[k], T.ly[me])
            rwait("ly", 0, 4, "r_yc")
        for x0, x1 in ch:
            step(0, x0, x1)
            step(1, x0, x1)
            if not last:
                spread("xw", x0, x1 - x0, 2048)
            else:
                c, x = x0 // 512, [("xw", x0, x1)]
                dma("ys", [(T.so[4 * c + a, 64 * s:64 * s + 64, :], T.xw[rows(s, a), x0:x1]) for s, a in SO if a != me], x, [("so", 4 * c, 4 * c + 4)])
                dma("y", [(T.yx[mine(s), x0:x1], T.xw[rows(s, me), x0:x1]) for s in range(2)], x, [])
                send("r_x%d" % c, ("so", 4 * c, 4 * c + 4), lambda k: T.so[4 * c + k], T.lo[4 * c + me])
                rwait("lo", 4 * c, 4 * c + 4, "r_x%d" % c)

    dma("y", [(T.yc[32 * k:32 * k + 32, :], T.ly[k]) for k in others], [("ly", 0, 4)], [])
    for c in range(4):
        dma("ys", [(T.yx[32 * k:32 * k + 32, 512 * c:512 * c + 512], T.lo[4 * c + k]) for k in others], [("lo", 4 * c, 4 * c + 4)], [])
    g.wait_ge(T.sem["r_loc"], nloc[0])
    for s in sorted(allsem):
        wait("y", (s, allsem[s]))
